import numpy as np
import ml_dtypes


def mxq(x, axis, fmt="e4m3"):
    dtype, down = {"e4m3": (ml_dtypes.float8_e4m3fn, 7), "e5m2": (ml_dtypes.float8_e5m2, 14)}[fmt]
    v = np.moveaxis(np.asarray(x, np.float32).astype(ml_dtypes.bfloat16).astype(np.float64), axis, -1)
    blocks = v.reshape(v.shape[:-1] + (-1, 32))
    amax = np.abs(blocks).max(-1, keepdims=True)
    byte = np.maximum(np.where(amax > 0, np.frexp(amax)[1] - 1 + 127, 0) - down, 1)
    scale = np.exp2(byte - 127.0)
    codes = (blocks / scale).astype(np.float32).astype(dtype).astype(np.float64)
    return np.moveaxis((codes * scale).reshape(v.shape), -1, axis)


WIDE = False


def mx_kscale(k):
    if not WIDE:
        return np.ones(k)
    levels = np.array([10, -10, 5, -5, 0])
    if k % 512:
        return np.exp2(np.random.permutation(np.resize(levels, k // 32))).repeat(32)
    a = np.empty((k // 512, 16))
    for p in range(k // 512):
        a[p, :8] = np.random.permutation(np.resize(levels, 8))
        for g in range(8):
            far = levels[np.abs(levels - a[p, g]) >= 10]
            a[p, g + 8] = far[np.random.randint(len(far))]
    return np.exp2(a.ravel()).repeat(32)


def f64(x):
    return np.asarray(x).astype(np.float64)


def striped(idx):
    return np.tile(np.asarray(idx).reshape(-1, 16).T, (8, 1)).astype(np.uint16)


def unstriped(offs):
    return offs[:16].T.reshape(-1).astype(np.int64)


E2M1 = np.array([0.0, 0.5, 1.0, 1.5, 2.0, 3.0, 4.0, 6.0, -0.0, -0.5, -1.0, -1.5, -2.0, -3.0, -4.0, -6.0])


def pack_weight(w, fmt):
    k, n = w.shape
    w = f64(np.asarray(w, np.float32).astype(ml_dtypes.bfloat16)).reshape(k // 32, 32, n)
    amax = np.abs(w).max(1)
    if fmt == "e4m3":
        byte = np.frexp(amax)[1] - 1 + 127 - 7
    else:
        mant, ex = np.frexp(amax / 6.0)
        byte = np.where(mant > 0.5, ex, ex - 1) + 127
    byte = np.clip(np.where(amax > 0, byte, 1), 1, 254)
    scaled = (w * np.exp2(127.0 - byte)[:, None, :]).reshape(k, n).astype(np.float32)
    by_word = np.ascontiguousarray(scaled.reshape(k // 512, 128, 4, n).transpose(0, 1, 3, 2))
    if fmt == "e4m3":
        words = by_word.astype(ml_dtypes.float8_e4m3fn).view(np.uint8)
    else:
        c = by_word.astype(ml_dtypes.float4_e2m1fn).view(np.uint8) & 0xF
        words = (c[..., 0::2] | (c[..., 1::2] << 4)).reshape(k // 512, 128, 2 * n)
    return np.ascontiguousarray(words), np.ascontiguousarray(byte.astype(np.uint8).reshape(k // 512, 16, n))


def unpack_weight(words, scales, fmt):
    g, _, n = scales.shape
    words = np.ascontiguousarray(words).reshape(g, 128, n, -1)
    if fmt == "e4m3":
        vals = words.view(ml_dtypes.float8_e4m3fn).astype(np.float64)
    else:
        nib = np.empty((g, 128, n, 4), np.uint8)
        nib[..., 0::2] = words & 0xF
        nib[..., 1::2] = words >> 4
        vals = E2M1[nib]
    vals = vals * np.repeat(np.exp2(scales.astype(np.float64) - 127.0), 8, axis=1)[..., None]
    return vals.transpose(0, 1, 3, 2).reshape(g * 512, n)


D, T, U, I, J, G = 512, 1024, 1024, 256, 512, 32


def setup_inputs():
    n = np.random.standard_normal
    idx = np.random.permutation(T)[:I]
    idx2 = np.random.permutation(U)[:J]
    fd = mx_kscale(D)
    fj = mx_kscale(J)
    tj = np.ones(U)
    tj[idx2] = fj
    tabbp = pack_weight(n((D, U)) / fd[:, None], "e2m1")
    return {
        "taba": (n((D, T)) * 1 / np.sqrt(D) * fd[:, None]).astype(np.float32),
        "tabb_words": tabbp[0],
        "tabb_scales": tabbp[1],
        "aim": (np.random.uniform(0.3, 2.0, (I, G))).astype(np.float32),
        "js": (np.random.uniform(4.0, 16.0, (1, J)) * fj).astype(np.float32),
        "brows": (n((D, U)) / tj).astype(np.float32),
        "old": (n((D, T)) * 2.0).astype(np.float32),
        "fade": (np.random.uniform(0.5, 1.0, (1, T))).astype(np.float32),
        "offs": striped(idx),
        "offs2": striped(idx2),
    }


def reference(taba, tabb_words, tabb_scales, aim, js, brows, old, fade, offs, offs2):
    idx = unstriped(offs)
    idx2 = unstriped(offs2)
    tabbu = unpack_weight(tabb_words, tabb_scales, "e2m1")
    tabaidxq = mxq(f64(taba)[:, idx], 0, "e4m3")
    tabbidx2g = tabbu[:, idx2]
    s = tabaidxq.T @ tabbidx2g
    v1 = np.sqrt(np.square(s).reshape(I, G, J // G).mean(axis=2) + 0.05)
    dv1 = (v1 - f64(aim)) * 2.0
    e1 = dv1 * 0.5 / np.sqrt(np.square(s).reshape(I, G, J // G).mean(axis=2) + 0.05) / 16.0
    r1 = np.repeat(e1, J // G, axis=1)
    ds = r1 * s * 2.0
    gs = ds * f64(js)
    gt1 = gs.T
    bt = f64(brows)[:, idx2].T
    btq = mxq(bt, 0, "e4m3")
    gt1q = mxq(gt1, 0, "e4m3")
    gx1 = btq.T @ gt1q
    gf = np.zeros((D, T))
    gf[:, idx] = gx1
    y = f64(old) * f64(fade) + gf
    return y

@@ -1,0 +1,189 @@
+from contextlib import ExitStack
+
+import concourse.mybir as mybir
+from concourse.masks import make_identity
+
+D, T, U, I, J, G = 512, 1024, 1024, 256, 512, 32
+FLOPS = 2 * 2 * D * I * J
+
+F32 = mybir.dt.float32
+BF16 = mybir.dt.bfloat16
+I32 = mybir.dt.int32
+U32 = mybir.dt.uint32
+U16 = mybir.dt.uint16
+U8 = mybir.dt.uint8
+FP8X4 = mybir.dt.float8_e4m3fn_x4
+FP4X4 = mybir.dt.float4_e2m1fn_x4
+ALU = mybir.AluOpType
+ACT = mybir.ActivationFunctionType
+AXIS = mybir.AxisListType
+
+P = 128
+PACK = 4
+GROUP = J // G
+I_TILES = I // P
+D_TILES = D // P
+BANK = 512
+
+
+def tile_attend_bgroupspread_x_kernel(tc, taba, tabb_words, tabb_scales, aim, js, brows, old, fade, offs, offs2, out):
+    nc = tc.nc
+    with ExitStack() as ctx:
+        held = ctx.enter_context(tc.tile_pool(name="held", bufs=1))
+        psum = ctx.enter_context(tc.psum_pool(name="psum", bufs=1))
+
+        def sbuf(name, shape, dtype):
+            return held.tile(shape, dtype, name=name, align_bytes=64)
+
+        def bank(number, name, shape):
+            return psum.tile(shape, F32, name=name, tag="bank%d" % number)
+
+        b_scales = sbuf("b_scales", [P, U], U8)
+        nc.gpsimd.memset(b_scales[:].bitcast(I32), 0)
+        for q in range(4):
+            nc.scalar.dma_start(b_scales[32 * q : 32 * q + 4, :].bitcast(I32), tabb_scales[0, 4 * q : 4 * q + 4, :].bitcast(I32))
+        identity = sbuf("identity", [P, P], F32)
+        make_identity(nc, identity[:])
+        idx = held.tile([P, I // 16], U16, name="idx")
+        idx2 = held.tile([P, J // 16], U16, name="idx2")
+        b_words = sbuf("b_words", [P, U], U16)
+        nc.sync.dma_start(idx2[:], offs2)
+        nc.sync.dma_start(b_words[:].bitcast(I32), tabb_words[0].bitcast(I32))
+        nc.sync.dma_start(idx[:], offs)
+        fade_cols = sbuf("fade_cols", [P, 2, PACK], F32)
+        nc.scalar.dma_start(fade_cols[:], fade.rearrange("o (h p c) -> p (o h) c", h=2, c=PACK))
+
+        a_planes = [sbuf("a_plane%d" % t, [P, T], F32) for t in range(PACK)]
+        taba_planes = taba.rearrange("(p t) c -> t p c", t=PACK)
+        for t in range(PACK):
+            nc.sync.dma_start(a_planes[t][:], taba_planes[t])
+
+        aim_sb = sbuf("aim_sb", [P, I_TILES, G], F32)
+        js_cols = sbuf("js_cols", [P, PACK], F32)
+        b_rows = [sbuf("b_rows%d" % m, [P, U], F32) for m in range(D_TILES)]
+        old_rows = [sbuf("old_rows%d" % m, [P, T], F32) for m in range(D_TILES)]
+        for m in range(D_TILES):
+            nc.sync.dma_start(b_rows[m][:], brows[m * P : (m + 1) * P, :])
+            if m == 0:
+                nc.sync.dma_start(aim_sb[:], aim.rearrange("(h p) g -> p h g", p=P))
+            if m == 1:
+                nc.sync.dma_start(js_cols[:], js.rearrange("o (p t) -> p (o t)", t=PACK))
+        for m in range(D_TILES):
+            nc.sync.dma_start(old_rows[m][:], old[m * P : (m + 1) * P, :])
+
+        placed = [sbuf("placed%d" % m, [P, T], F32) for m in range(D_TILES)]
+        for m in range(D_TILES):
+            nc.vector.memset(placed[m][:], 0.0)
+
+        fade_banks = [bank(6 + h, "fade_bank%d" % h, [P, PACK, P]) for h in range(2)]
+        for h in range(2):
+            for c in range(PACK):
+                nc.tensor.transpose(fade_banks[h][:, c, :], fade_cols[:, h, c : c + 1].to_broadcast([P, P]), identity[:])
+
+        bg_words = sbuf("bg_words", [P, J], U16)
+        nc.vector.tensor_copy(bg_words[:], b_words[:].indirect(idx2[:]))
+        bg_scales = sbuf("bg_scales", [P, J], U8)
+        nc.vector.tensor_copy(bg_scales[:], b_scales[:].indirect(idx2[:]))
+
+        a_picked = sbuf("a_picked", [P, PACK, I], BF16)
+        for t in range(PACK):
+            nc.scalar.activation(a_picked[:, t, :], a_planes[t][:].indirect(idx[:]), ACT.Copy)
+
+        aim_scaled = sbuf("aim_scaled", [P, I_TILES, G], F32)
+        nc.vector.tensor_scalar(aim_scaled[:], aim_sb[:], -0.125, None, ALU.mult)
+
+        scores = []
+        for h in range(I_TILES):
+            a_woven = sbuf("a_woven%d" % h, [P, P, PACK], BF16)
+            nc.vector.tensor_copy(a_woven[:], a_picked[:, :, h * P : (h + 1) * P].rearrange("p t i -> p i t"))
+            a_codes = sbuf("a_codes%d" % h, [P, P], U32)
+            a_scales = sbuf("a_scales%d" % h, [P, P], U8)
+            nc.vector.quantize_mx(out=a_codes[:].bitcast(FP8X4), scales=a_scales[:], in_=a_woven[:].rearrange("p i t -> p (i t)"))
+            score = bank(h, "score%d" % h, [P, J])
+            nc.tensor.matmul_mx(
+                out=score[:], lhsT=a_codes[:].bitcast(FP8X4), lhsT_scale=a_scales[:],
+                rhs=bg_words[:].bitcast(U8).bitcast(FP4X4), rhs_scale=bg_scales[:], start=True, stop=True,
+            )
+            scores.append(score)
+
+        g_codes = sbuf("g_codes", [P, I], U32)
+        g_scales = sbuf("g_scales", [P, I], U8)
+        squares = [sbuf("squares%d" % h, [P, J], F32) for h in range(I_TILES)]
+        sums = [sbuf("sums%d" % h, [P, G], F32) for h in range(I_TILES)]
+        inv = [sbuf("inv%d" % h, [P, G], F32) for h in range(I_TILES)]
+        ratio = [sbuf("ratio%d" % h, [P, G], F32) for h in range(I_TILES)]
+        slope = [sbuf("slope%d" % h, [P, G], F32) for h in range(I_TILES)]
+        ds = [sbuf("ds%d" % h, [P, PACK, P], F32) for h in range(I_TILES)]
+        g_woven = [sbuf("g_woven%d" % h, [P, P, PACK], BF16) for h in range(I_TILES)]
+        ds_turned = [bank(2 + h, "ds_turned%d" % h, [P, PACK, P]) for h in range(I_TILES)]
+        for h in range(I_TILES):
+            nc.scalar.activation(squares[h][:], scores[h][:], ACT.Square)
+        for h in range(I_TILES):
+            nc.vector.tensor_reduce(sums[h][:], squares[h][:].rearrange("p (g e) -> p g e", e=GROUP), AXIS.X, ALU.add)
+        for h in range(I_TILES):
+            nc.scalar.activation(inv[h][:], sums[h][:], ACT.Abs_reciprocal_sqrt, bias=0.05, scale=1.0 / GROUP)
+        for h in range(I_TILES):
+            nc.vector.tensor_tensor(ratio[h][:], inv[h][:], aim_scaled[:, h, :], ALU.mult)
+        for h in range(I_TILES):
+            nc.vector.tensor_scalar(slope[h][:], ratio[h][:], 0.125, None, ALU.add)
+        for h in range(I_TILES):
+            nc.vector.tensor_tensor(
+                ds[h][:].rearrange("p t (g r) -> p t g r", g=G),
+                scores[h][:].rearrange("p (g r t) -> p t g r", g=G, t=PACK),
+                slope[h][:].unsqueeze(1).unsqueeze(3).to_broadcast([P, PACK, G, GROUP // PACK]),
+                ALU.mult,
+            )
+        for h in range(I_TILES):
+            for t in range(PACK):
+                nc.tensor.transpose(ds_turned[h][:, t, :], ds[h][:, t, :], identity[:])
+        for h in range(I_TILES):
+            nc.vector.tensor_tensor(
+                g_woven[h][:],
+                ds_turned[h][:].rearrange("p t i -> p i t"),
+                js_cols[:].unsqueeze(1).to_broadcast([P, P, PACK]),
+                ALU.mult,
+            )
+        for h in range(I_TILES):
+            cols = slice(h * P, (h + 1) * P)
+            nc.vector.quantize_mx(out=g_codes[:, cols].bitcast(FP8X4), scales=g_scales[:, cols], in_=g_woven[h][:].rearrange("p i t -> p (i t)"))
+
+        bt_codes = [sbuf("bt_codes%d" % m, [P, P], U32) for m in range(D_TILES)]
+        bt_scales = [sbuf("bt_scales%d" % m, [P, P], U8) for m in range(D_TILES)]
+        for m in range(D_TILES):
+            picked = sbuf("b_picked%d" % m, [P, J], BF16)
+            nc.scalar.activation(picked[:], b_rows[m][:].indirect(idx2[:]), ACT.Copy)
+            pairs = picked[:].bitcast(F32)
+            turned = bank(4 + m % 2, "b_turned%d" % m, [P, 2, P])
+            for u in range(2):
+                nc.tensor.transpose(turned[:, u, :], pairs[:, u : J // 2 : 2], identity[:])
+            woven = sbuf("b_woven%d" % m, [P, P, 2], F32)
+            nc.scalar.copy(woven[:], turned[:].rearrange("p u d -> p d u"))
+            nc.vector.quantize_mx(out=bt_codes[m][:].bitcast(FP8X4), scales=bt_scales[m][:], in_=woven[:].rearrange("p d u -> p (d u)").bitcast(BF16))
+
+        for m in range(D_TILES):
+            grad = bank(m, "grad%d" % m, [P, I])
+            nc.tensor.matmul_mx(
+                out=grad[:], lhsT=bt_codes[m][:].bitcast(FP8X4), lhsT_scale=bt_scales[m][:],
+                rhs=g_codes[:].bitcast(FP8X4), rhs_scale=g_scales[:], start=True, stop=True,
+            )
+            grad_sb = sbuf("grad_sb%d" % m, [P, I], F32)
+            if m == 1:
+                nc.vector.tensor_copy(grad_sb[:], grad[:])
+                nc.vector.tensor_copy(placed[m][:].indirect(idx[:]), grad_sb[:])
+            else:
+                nc.scalar.copy(grad_sb[:], grad[:])
+                nc.scalar.activation(placed[m][:].indirect(idx[:]), grad_sb[:], ACT.Copy)
+
+        for m in range(D_TILES):
+            for h in range(2):
+                cols = slice(h * BANK, (h + 1) * BANK)
+                faded = sbuf("faded%d_%d" % (m, h), [P, BANK], F32)
+                nc.vector.tensor_tensor(
+                    faded[:].rearrange("p (n c) -> p n c", c=PACK),
+                    fade_banks[h][:].rearrange("p c n -> p n c"),
+                    old_rows[m][:, cols].rearrange("p (n c) -> p n c", c=PACK),
+                    ALU.mult,
+                )
+                result = sbuf("result%d_%d" % (m, h), [P, BANK], F32)
+                nc.vector.tensor_tensor(result[:], faded[:], placed[m][:, cols], ALU.add)
+                nc.sync.dma_start(out[m * P : (m + 1) * P, cols], result[:])

@@ -20,10 +20,22 @@ AXIS = mybir.AxisListType
 
 P = 128
 PACK = 4
+QUADRANT = 32
+LIST_ROWS = 16
 GROUP = J // G
+GROUP_ROWS = GROUP // PACK
 I_TILES = I // P
 D_TILES = D // P
 BANK = 512
+T_HALVES = T // BANK
+SLOPE = 2.0 * 0.5 / GROUP * 2.0
+EPSILON = 0.05
+
+SCORE_BANKS = (0, 1)
+SUM_BANKS = (2, 3)
+RATIO_BANK = 0
+FADE_BANKS = (6, 7)
+GRAD_BANKS = (1, 4, 3, 0)
 
 
 def tile_attend_bgroupspread_x_kernel(tc, taba, tabb_words, tabb_scales, aim, js, brows, old, fade, offs, offs2, out):
@@ -32,158 +44,203 @@ def tile_attend_bgroupspread_x_kernel(tc, taba, tabb_words, tabb_scales, aim, js
         held = ctx.enter_context(tc.tile_pool(name="held", bufs=1))
         psum = ctx.enter_context(tc.psum_pool(name="psum", bufs=1))
 
-        def sbuf(name, shape, dtype):
-            return held.tile(shape, dtype, name=name, align_bytes=64)
+        def sbuf(name, shape, dtype, buffer_of=None):
+            return held.tile(shape, dtype, name=name, tag=buffer_of or name, align_bytes=64)
 
         def bank(number, name, shape):
             return psum.tile(shape, F32, name=name, tag="bank%d" % number)
 
         b_scales = sbuf("b_scales", [P, U], U8)
         nc.gpsimd.memset(b_scales[:].bitcast(I32), 0)
-        for q in range(4):
-            nc.scalar.dma_start(b_scales[32 * q : 32 * q + 4, :].bitcast(I32), tabb_scales[0, 4 * q : 4 * q + 4, :].bitcast(I32))
+        for q in range(P // QUADRANT):
+            nc.scalar.dma_start(
+                b_scales[QUADRANT * q : QUADRANT * q + 4, :].bitcast(I32),
+                tabb_scales[0, 4 * q : 4 * q + 4, :].bitcast(I32),
+            )
         identity = sbuf("identity", [P, P], F32)
         make_identity(nc, identity[:])
-        idx = held.tile([P, I // 16], U16, name="idx")
-        idx2 = held.tile([P, J // 16], U16, name="idx2")
+        idx = held.tile([P, I // LIST_ROWS], U16, name="idx")
+        idx2 = held.tile([P, J // LIST_ROWS], U16, name="idx2")
         b_words = sbuf("b_words", [P, U], U16)
         nc.sync.dma_start(idx2[:], offs2)
         nc.sync.dma_start(b_words[:].bitcast(I32), tabb_words[0].bitcast(I32))
         nc.sync.dma_start(idx[:], offs)
-        fade_cols = sbuf("fade_cols", [P, 2, PACK], F32)
-        nc.scalar.dma_start(fade_cols[:], fade.rearrange("o (h p c) -> p (o h) c", h=2, c=PACK))
+        fade_cols = sbuf("fade_cols", [P, T_HALVES, PACK], F32)
+        nc.scalar.dma_start(fade_cols[:], fade.rearrange("o (h p c) -> p (o h) c", h=T_HALVES, c=PACK))
 
-        a_planes = [sbuf("a_plane%d" % t, [P, T], F32) for t in range(PACK)]
-        taba_planes = taba.rearrange("(p t) c -> t p c", t=PACK)
+        a_rows = [sbuf("a_rows%d" % t, [P, T], F32) for t in range(PACK)]
+        taba_by_place = taba.rearrange("(p t) c -> t p c", t=PACK)
         for t in range(PACK):
-            nc.sync.dma_start(a_planes[t][:], taba_planes[t])
+            nc.sync.dma_start(a_rows[t][:], taba_by_place[t])
 
         aim_sb = sbuf("aim_sb", [P, I_TILES, G], F32)
         js_cols = sbuf("js_cols", [P, PACK], F32)
         b_rows = [sbuf("b_rows%d" % m, [P, U], F32) for m in range(D_TILES)]
         old_rows = [sbuf("old_rows%d" % m, [P, T], F32) for m in range(D_TILES)]
-        for m in range(D_TILES):
-            nc.sync.dma_start(b_rows[m][:], brows[m * P : (m + 1) * P, :])
-            if m == 0:
-                nc.sync.dma_start(aim_sb[:], aim.rearrange("(h p) g -> p h g", p=P))
-            if m == 1:
-                nc.sync.dma_start(js_cols[:], js.rearrange("o (p t) -> p (o t)", t=PACK))
-        for m in range(D_TILES):
-            nc.sync.dma_start(old_rows[m][:], old[m * P : (m + 1) * P, :])
+
+        def load_rows(tiles, source, m):
+            nc.sync.dma_start(tiles[m][:], source[m * P : (m + 1) * P, :])
+
+        load_rows(b_rows, brows, 0)
+        nc.sync.dma_start(aim_sb[:], aim.rearrange("(h p) g -> p h g", p=P))
+        load_rows(b_rows, brows, 1)
+        nc.sync.dma_start(js_cols[:], js.rearrange("o (p t) -> p (o t)", t=PACK))
+        load_rows(old_rows, old, 0)
+        for m in range(2, D_TILES):
+            load_rows(b_rows, brows, m)
+        for m in range(1, D_TILES):
+            load_rows(old_rows, old, m)
 
         placed = [sbuf("placed%d" % m, [P, T], F32) for m in range(D_TILES)]
-        for m in range(D_TILES):
-            nc.vector.memset(placed[m][:], 0.0)
 
-        fade_banks = [bank(6 + h, "fade_bank%d" % h, [P, PACK, P]) for h in range(2)]
-        for h in range(2):
+        fade_rows = [bank(FADE_BANKS[h], "fade_rows%d" % h, [P, PACK, P]) for h in range(T_HALVES)]
+        for h in range(T_HALVES):
             for c in range(PACK):
-                nc.tensor.transpose(fade_banks[h][:, c, :], fade_cols[:, h, c : c + 1].to_broadcast([P, P]), identity[:])
+                nc.tensor.transpose(fade_rows[h][:, c, :], fade_cols[:, h, c : c + 1].to_broadcast([P, P]), identity[:])
 
-        bg_words = sbuf("bg_words", [P, J], U16)
-        nc.vector.tensor_copy(bg_words[:], b_words[:].indirect(idx2[:]))
-        bg_scales = sbuf("bg_scales", [P, J], U8)
-        nc.vector.tensor_copy(bg_scales[:], b_scales[:].indirect(idx2[:]))
+        picked_words = sbuf("picked_words", [P, J], U16)
+        nc.vector.tensor_copy(picked_words[:], b_words[:].indirect(idx2[:]))
+        dealt_words = sbuf("dealt_words", [P, PACK, P], U16)
+        dealt_scales = sbuf("dealt_scales", [P, PACK, P], U8)
+        nc.vector.tensor_copy(dealt_scales[:].rearrange("p t q -> p q t"), b_scales[:].indirect(idx2[:]))
+        nc.vector.tensor_copy(dealt_words[:], picked_words[:].rearrange("p (q t) -> p t q", t=PACK))
 
         a_picked = sbuf("a_picked", [P, PACK, I], BF16)
-        for t in range(PACK):
-            nc.scalar.activation(a_picked[:, t, :], a_planes[t][:].indirect(idx[:]), ACT.Copy)
+        last = PACK - 1
+        for t in range(last):
+            nc.scalar.activation(a_picked[:, t, :], a_rows[t][:].indirect(idx[:]), ACT.Copy)
+        nc.vector.tensor_copy(a_picked[:, last, 0:P], a_rows[last][:].indirect(idx[:, 0 : P // LIST_ROWS]))
+        nc.scalar.activation(a_picked[:, last, P:I], a_rows[last][:].indirect(idx[:, P // LIST_ROWS : I // LIST_ROWS]), ACT.Copy)
 
+        for m in range(D_TILES):
+            nc.vector.memset(placed[m][:], 0.0)
         aim_scaled = sbuf("aim_scaled", [P, I_TILES, G], F32)
-        nc.vector.tensor_scalar(aim_scaled[:], aim_sb[:], -0.125, None, ALU.mult)
+        nc.vector.tensor_scalar(aim_scaled[:], aim_sb[:], -SLOPE, None, ALU.mult)
 
-        scores = []
-        for h in range(I_TILES):
-            a_woven = sbuf("a_woven%d" % h, [P, P, PACK], BF16)
-            nc.vector.tensor_copy(a_woven[:], a_picked[:, :, h * P : (h + 1) * P].rearrange("p t i -> p i t"))
-            a_codes = sbuf("a_codes%d" % h, [P, P], U32)
-            a_scales = sbuf("a_scales%d" % h, [P, P], U8)
-            nc.vector.quantize_mx(out=a_codes[:].bitcast(FP8X4), scales=a_scales[:], in_=a_woven[:].rearrange("p i t -> p (i t)"))
-            score = bank(h, "score%d" % h, [P, J])
+        i_tiles = [slice(h * P, (h + 1) * P) for h in range(I_TILES)]
+        a_woven = sbuf("a_woven", [P, I, PACK], BF16)
+        for cols in i_tiles:
+            nc.vector.tensor_copy(a_woven[:, cols, :], a_picked[:, :, cols].rearrange("p t i -> p i t"))
+        a_codes = sbuf("a_codes", [P, I], U32)
+        a_scales = sbuf("a_scales", [P, I], U8)
+        nc.vector.quantize_mx(out=a_codes[:].bitcast(FP8X4), scales=a_scales[:], in_=a_woven[:].rearrange("p i t -> p (i t)"))
+
+        scores = [bank(number, "scores%d" % u, [P, 2, I]) for u, number in enumerate(SCORE_BANKS)]
+        for t in range(PACK):
             nc.tensor.matmul_mx(
-                out=score[:], lhsT=a_codes[:].bitcast(FP8X4), lhsT_scale=a_scales[:],
-                rhs=bg_words[:].bitcast(U8).bitcast(FP4X4), rhs_scale=bg_scales[:], start=True, stop=True,
+                out=scores[t // 2][:, t % 2, :],
+                lhsT=dealt_words[:, t, :].bitcast(U8).bitcast(FP4X4),
+                lhsT_scale=dealt_scales[:, t, :],
+                rhs=a_codes[:].bitcast(FP8X4),
+                rhs_scale=a_scales[:],
+                start=True,
+                stop=True,
             )
-            scores.append(score)
 
+        squares = sbuf("squares", [P, PACK, I], F32)
+        for u in range(len(scores)):
+            nc.scalar.activation(squares[:, 2 * u : 2 * u + 2, :], scores[u][:], ACT.Square)
+        square_sums = [bank(SUM_BANKS[h], "square_sums%d" % h, [P, P]) for h in range(I_TILES)]
+        for t in range(PACK):
+            for h in range(I_TILES):
+                nc.tensor.matmul(
+                    square_sums[h][:], squares[:, t, i_tiles[h]], identity[:], start=(t == 0), stop=(t == last), is_transpose=True
+                )
+        sums = sbuf("sums", [P, I_TILES, G], F32)
+        for h in range(I_TILES):
+            nc.vector.tensor_reduce(sums[:, h, :], square_sums[h][:].rearrange("p (g r) -> p g r", g=G), AXIS.X, ALU.add)
+        scaled = sbuf("scaled", [P, PACK, I], F32)
+        for t in range(PACK):
+            nc.scalar.activation(scaled[:, t, :], scores[t // 2][:, t % 2, :], ACT.Copy, scale=js_cols[:, t : t + 1])
+        inv_spread = sbuf("inv_spread", [P, I_TILES, G], F32)
+        nc.scalar.activation(inv_spread[:], sums[:], ACT.Abs_reciprocal_sqrt, bias=EPSILON, scale=1.0 / GROUP)
+        ratio_shape = [P, I_TILES * G, GROUP_ROWS]
+        ratio = sbuf("ratio", ratio_shape, F32)
+        nc.vector.tensor_tensor(
+            ratio[:],
+            inv_spread[:].rearrange("p h g -> p (h g)").unsqueeze(2).to_broadcast(ratio_shape),
+            aim_scaled[:].rearrange("p h g -> p (h g)").unsqueeze(2).to_broadcast(ratio_shape),
+            ALU.mult,
+        )
+        ratio_turned = bank(RATIO_BANK, "ratio_turned", [P, I])
+        ratio_flat = ratio[:].rearrange("p c r -> p (c r)")
+        for cols in i_tiles:
+            nc.tensor.transpose(ratio_turned[:, cols], ratio_flat[:, cols], identity[:])
+
+        g_woven = sbuf("g_woven", [P, I, PACK], BF16)
+        for cols in i_tiles:
+            nc.vector.scalar_tensor_tensor(
+                g_woven[:, cols, :],
+                ratio_turned[:, cols].unsqueeze(2).to_broadcast([P, P, PACK]),
+                SLOPE,
+                scaled[:, :, cols].rearrange("p t i -> p i t"),
+                ALU.add,
+                ALU.mult,
+            )
         g_codes = sbuf("g_codes", [P, I], U32)
         g_scales = sbuf("g_scales", [P, I], U8)
-        squares = [sbuf("squares%d" % h, [P, J], F32) for h in range(I_TILES)]
-        sums = [sbuf("sums%d" % h, [P, G], F32) for h in range(I_TILES)]
-        inv = [sbuf("inv%d" % h, [P, G], F32) for h in range(I_TILES)]
-        ratio = [sbuf("ratio%d" % h, [P, G], F32) for h in range(I_TILES)]
-        slope = [sbuf("slope%d" % h, [P, G], F32) for h in range(I_TILES)]
-        ds = [sbuf("ds%d" % h, [P, PACK, P], F32) for h in range(I_TILES)]
-        g_woven = [sbuf("g_woven%d" % h, [P, P, PACK], BF16) for h in range(I_TILES)]
-        ds_turned = [bank(2 + h, "ds_turned%d" % h, [P, PACK, P]) for h in range(I_TILES)]
-        for h in range(I_TILES):
-            nc.scalar.activation(squares[h][:], scores[h][:], ACT.Square)
-        for h in range(I_TILES):
-            nc.vector.tensor_reduce(sums[h][:], squares[h][:].rearrange("p (g e) -> p g e", e=GROUP), AXIS.X, ALU.add)
-        for h in range(I_TILES):
-            nc.scalar.activation(inv[h][:], sums[h][:], ACT.Abs_reciprocal_sqrt, bias=0.05, scale=1.0 / GROUP)
-        for h in range(I_TILES):
-            nc.vector.tensor_tensor(ratio[h][:], inv[h][:], aim_scaled[:, h, :], ALU.mult)
-        for h in range(I_TILES):
-            nc.vector.tensor_scalar(slope[h][:], ratio[h][:], 0.125, None, ALU.add)
-        for h in range(I_TILES):
-            nc.vector.tensor_tensor(
-                ds[h][:].rearrange("p t (g r) -> p t g r", g=G),
-                scores[h][:].rearrange("p (g r t) -> p t g r", g=G, t=PACK),
-                slope[h][:].unsqueeze(1).unsqueeze(3).to_broadcast([P, PACK, G, GROUP // PACK]),
-                ALU.mult,
+        for cols in i_tiles:
+            nc.vector.quantize_mx(
+                out=g_codes[:, cols].bitcast(FP8X4), scales=g_scales[:, cols], in_=g_woven[:, cols, :].rearrange("p i t -> p (i t)")
             )
-        for h in range(I_TILES):
-            for t in range(PACK):
-                nc.tensor.transpose(ds_turned[h][:, t, :], ds[h][:, t, :], identity[:])
-        for h in range(I_TILES):
-            nc.vector.tensor_tensor(
-                g_woven[h][:],
-                ds_turned[h][:].rearrange("p t i -> p i t"),
-                js_cols[:].unsqueeze(1).to_broadcast([P, P, PACK]),
-                ALU.mult,
-            )
-        for h in range(I_TILES):
-            cols = slice(h * P, (h + 1) * P)
-            nc.vector.quantize_mx(out=g_codes[:, cols].bitcast(FP8X4), scales=g_scales[:, cols], in_=g_woven[h][:].rearrange("p i t -> p (i t)"))
 
-        bt_codes = [sbuf("bt_codes%d" % m, [P, P], U32) for m in range(D_TILES)]
-        bt_scales = [sbuf("bt_scales%d" % m, [P, P], U8) for m in range(D_TILES)]
-        for m in range(D_TILES):
-            picked = sbuf("b_picked%d" % m, [P, J], BF16)
-            nc.scalar.activation(picked[:], b_rows[m][:].indirect(idx2[:]), ACT.Copy)
-            pairs = picked[:].bitcast(F32)
-            turned = bank(4 + m % 2, "b_turned%d" % m, [P, 2, P])
-            for u in range(2):
-                nc.tensor.transpose(turned[:, u, :], pairs[:, u : J // 2 : 2], identity[:])
-            woven = sbuf("b_woven%d" % m, [P, P, 2], F32)
-            nc.scalar.copy(woven[:], turned[:].rearrange("p u d -> p d u"))
-            nc.vector.quantize_mx(out=bt_codes[m][:].bitcast(FP8X4), scales=bt_scales[m][:], in_=woven[:].rearrange("p d u -> p (d u)").bitcast(BF16))
+        bt_woven = [sbuf("bt_woven%d" % pair, [P, 2, P, 2], F32) for pair in range(D_TILES // 2)]
+        bt_codes = sbuf("bt_codes", [P, D], U32, buffer_of="scaled")
+        bt_scales = sbuf("bt_scales", [P, D], U8)
+        for first, count, buffer_of, number in ((0, 2, None, 4), (2, 1, "sums", 5), (3, 1, "bt_woven0", 4)):
+            picked = sbuf("b_picked%d" % first, [P, count, J], BF16, buffer_of=buffer_of)
+            turned = bank(number, "b_turned%d" % first, [P, count, 2, P])
+            for e in range(count):
+                m = first + e
+                if m % 2 == 1:
+                    nc.vector.tensor_copy(picked[:, e, :], b_rows[m][:].indirect(idx2[:]))
+                else:
+                    nc.scalar.activation(picked[:, e, :], b_rows[m][:].indirect(idx2[:]), ACT.Copy)
+            for e in range(count):
+                words = picked[:, e, :].bitcast(F32)
+                for u in range(2):
+                    nc.tensor.transpose(turned[:, e, u, :], words[:, u : J // 2 : 2], identity[:])
+            pair = first // 2
+            nc.scalar.copy(bt_woven[pair][:, first % 2 : first % 2 + count], turned[:].rearrange("p e u d -> p e d u"))
+            if (first + count) % 2 == 0:
+                rows = slice(2 * pair * P, 2 * (pair + 1) * P)
+                nc.vector.quantize_mx(
+                    out=bt_codes[:, rows].bitcast(FP8X4),
+                    scales=bt_scales[:, rows],
+                    in_=bt_woven[pair][:].rearrange("p e d u -> p (e d u)").bitcast(BF16),
+                )
 
         for m in range(D_TILES):
-            grad = bank(m, "grad%d" % m, [P, I])
+            grad = bank(GRAD_BANKS[m], "grad%d" % m, [P, I])
+            rows = slice(m * P, (m + 1) * P)
             nc.tensor.matmul_mx(
-                out=grad[:], lhsT=bt_codes[m][:].bitcast(FP8X4), lhsT_scale=bt_scales[m][:],
-                rhs=g_codes[:].bitcast(FP8X4), rhs_scale=g_scales[:], start=True, stop=True,
+                out=grad[:],
+                lhsT=bt_codes[:, rows].bitcast(FP8X4),
+                lhsT_scale=bt_scales[:, rows],
+                rhs=g_codes[:].bitcast(FP8X4),
+                rhs_scale=g_scales[:],
+                start=True,
+                stop=True,
             )
             grad_sb = sbuf("grad_sb%d" % m, [P, I], F32)
-            if m == 1:
-                nc.vector.tensor_copy(grad_sb[:], grad[:])
-                nc.vector.tensor_copy(placed[m][:].indirect(idx[:]), grad_sb[:])
-            else:
-                nc.scalar.copy(grad_sb[:], grad[:])
-                nc.scalar.activation(placed[m][:].indirect(idx[:]), grad_sb[:], ACT.Copy)
+            nc.scalar.copy(grad_sb[:], grad[:])
+            nc.scalar.activation(placed[m][:].indirect(idx[:]), grad_sb[:], ACT.Copy)
 
+        faded = [sbuf("faded%d" % m, [P, T], F32) for m in range(D_TILES)]
         for m in range(D_TILES):
-            for h in range(2):
+            for h in range(T_HALVES):
                 cols = slice(h * BANK, (h + 1) * BANK)
-                faded = sbuf("faded%d_%d" % (m, h), [P, BANK], F32)
                 nc.vector.tensor_tensor(
-                    faded[:].rearrange("p (n c) -> p n c", c=PACK),
-                    fade_banks[h][:].rearrange("p c n -> p n c"),
+                    faded[m][:, cols].rearrange("p (n c) -> p n c", c=PACK),
+                    fade_rows[h][:].rearrange("p c n -> p n c"),
                     old_rows[m][:, cols].rearrange("p (n c) -> p n c", c=PACK),
                     ALU.mult,
                 )
-                result = sbuf("result%d_%d" % (m, h), [P, BANK], F32)
-                nc.vector.tensor_tensor(result[:], faded[:], placed[m][:, cols], ALU.add)
+        for m in range(D_TILES):
+            pieces = 2 if m == D_TILES - 1 else 1
+            width = T // pieces
+            for piece in range(pieces):
+                cols = slice(piece * width, (piece + 1) * width)
+                result = sbuf("result%d_%d" % (m, piece), [P, width], F32)
+                nc.vector.tensor_tensor(result[:], faded[m][:, cols], placed[m][:, cols], ALU.add)
                 nc.sync.dma_start(out[m * P : (m + 1) * P, cols], result[:])

@@ -57,6 +57,10 @@ def tile_attend_bgroupspread_x_kernel(tc, taba, tabb_words, tabb_scales, aim, js
                 b_scales[QUADRANT * q : QUADRANT * q + 4, :].bitcast(I32),
                 tabb_scales[0, 4 * q : 4 * q + 4, :].bitcast(I32),
             )
+        warm_in = sbuf("warm_in", [P, 1], F32)
+        warm_out = sbuf("warm_out", [P, 1], F32)
+        nc.vector.memset(warm_in[:], 1.0)
+        nc.scalar.activation(warm_out[:], warm_in[:], ACT.Abs_reciprocal_sqrt)
         identity = sbuf("identity", [P, P], F32)
         make_identity(nc, identity[:])
         idx = held.tile([P, I // LIST_ROWS], U16, name="idx")

from contextlib import ExitStack

import concourse.mybir as mybir
from concourse.masks import make_identity

D, T, U, I, J, G = 512, 1024, 1024, 256, 512, 32
FLOPS = 2 * 2 * D * I * J

F32 = mybir.dt.float32
BF16 = mybir.dt.bfloat16
I32 = mybir.dt.int32
U32 = mybir.dt.uint32
U16 = mybir.dt.uint16
U8 = mybir.dt.uint8
FP8X4 = mybir.dt.float8_e4m3fn_x4
FP4X4 = mybir.dt.float4_e2m1fn_x4
ALU = mybir.AluOpType
ACT = mybir.ActivationFunctionType
AXIS = mybir.AxisListType

P = 128
PACK = 4
QUADRANT = 32
LIST_ROWS = 16
GROUP = J // G
GROUP_ROWS = GROUP // PACK
I_TILES = I // P
D_TILES = D // P
BANK = 512
T_HALVES = T // BANK
SLOPE = 2.0 * 0.5 / GROUP * 2.0
EPSILON = 0.05

SCORE_BANKS = (0, 1)
SUM_BANKS = (2, 3)
RATIO_BANK = 0
FADE_BANKS = (6, 7)
GRAD_BANKS = (1, 4, 3, 0)


def tile_attend_bgroupspread_x_kernel(tc, taba, tabb_words, tabb_scales, aim, js, brows, old, fade, offs, offs2, out):
    nc = tc.nc
    with ExitStack() as ctx:
        held = ctx.enter_context(tc.tile_pool(name="held", bufs=1))
        psum = ctx.enter_context(tc.psum_pool(name="psum", bufs=1))

        def sbuf(name, shape, dtype, buffer_of=None):
            return held.tile(shape, dtype, name=name, tag=buffer_of or name, align_bytes=64)

        def bank(number, name, shape):
            return psum.tile(shape, F32, name=name, tag="bank%d" % number)

        b_scales = sbuf("b_scales", [P, U], U8)
        nc.gpsimd.memset(b_scales[:].bitcast(I32), 0)
        for q in range(P // QUADRANT):
            nc.scalar.dma_start(
                b_scales[QUADRANT * q : QUADRANT * q + 4, :].bitcast(I32),
                tabb_scales[0, 4 * q : 4 * q + 4, :].bitcast(I32),
            )
        warm_in = sbuf("warm_in", [P, 1], F32)
        warm_out = sbuf("warm_out", [P, 1], F32)
        nc.vector.memset(warm_in[:], 1.0)
        nc.scalar.activation(warm_out[:], warm_in[:], ACT.Abs_reciprocal_sqrt)
        identity = sbuf("identity", [P, P], F32)
        make_identity(nc, identity[:])
        idx = held.tile([P, I // LIST_ROWS], U16, name="idx")
        idx2 = held.tile([P, J // LIST_ROWS], U16, name="idx2")
        b_words = sbuf("b_words", [P, U], U16)
        nc.sync.dma_start(idx2[:], offs2)
        nc.sync.dma_start(b_words[:].bitcast(I32), tabb_words[0].bitcast(I32))
        nc.sync.dma_start(idx[:], offs)
        fade_cols = sbuf("fade_cols", [P, T_HALVES, PACK], F32)
        nc.scalar.dma_start(fade_cols[:], fade.rearrange("o (h p c) -> p (o h) c", h=T_HALVES, c=PACK))

        a_rows = [sbuf("a_rows%d" % t, [P, T], F32) for t in range(PACK)]
        taba_by_place = taba.rearrange("(p t) c -> t p c", t=PACK)
        for t in range(PACK):
            nc.sync.dma_start(a_rows[t][:], taba_by_place[t])

        aim_sb = sbuf("aim_sb", [P, I_TILES, G], F32)
        js_cols = sbuf("js_cols", [P, PACK], F32)
        b_rows = [sbuf("b_rows%d" % m, [P, U], F32) for m in range(D_TILES)]
        old_rows = [sbuf("old_rows%d" % m, [P, T], F32) for m in range(D_TILES)]

        def load_rows(tiles, source, m):
            nc.sync.dma_start(tiles[m][:], source[m * P : (m + 1) * P, :])

        load_rows(b_rows, brows, 0)
        nc.sync.dma_start(aim_sb[:], aim.rearrange("(h p) g -> p h g", p=P))
        load_rows(b_rows, brows, 1)
        nc.sync.dma_start(js_cols[:], js.rearrange("o (p t) -> p (o t)", t=PACK))
        load_rows(old_rows, old, 0)
        for m in range(2, D_TILES):
            load_rows(b_rows, brows, m)
        for m in range(1, D_TILES):
            load_rows(old_rows, old, m)

        placed = [sbuf("placed%d" % m, [P, T], F32) for m in range(D_TILES)]

        fade_rows = [bank(FADE_BANKS[h], "fade_rows%d" % h, [P, PACK, P]) for h in range(T_HALVES)]
        for h in range(T_HALVES):
            for c in range(PACK):
                nc.tensor.transpose(fade_rows[h][:, c, :], fade_cols[:, h, c : c + 1].to_broadcast([P, P]), identity[:])

        picked_words = sbuf("picked_words", [P, J], U16)
        nc.vector.tensor_copy(picked_words[:], b_words[:].indirect(idx2[:]))
        dealt_words = sbuf("dealt_words", [P, PACK, P], U16)
        dealt_scales = sbuf("dealt_scales", [P, PACK, P], U8)
        nc.vector.tensor_copy(dealt_scales[:].rearrange("p t q -> p q t"), b_scales[:].indirect(idx2[:]))
        nc.vector.tensor_copy(dealt_words[:], picked_words[:].rearrange("p (q t) -> p t q", t=PACK))

        a_picked = sbuf("a_picked", [P, PACK, I], BF16)
        last = PACK - 1
        for t in range(last):
            nc.scalar.activation(a_picked[:, t, :], a_rows[t][:].indirect(idx[:]), ACT.Copy)
        nc.vector.tensor_copy(a_picked[:, last, 0:P], a_rows[last][:].indirect(idx[:, 0 : P // LIST_ROWS]))
        nc.scalar.activation(a_picked[:, last, P:I], a_rows[last][:].indirect(idx[:, P // LIST_ROWS : I // LIST_ROWS]), ACT.Copy)

        for m in range(D_TILES):
            nc.vector.memset(placed[m][:], 0.0)
        aim_scaled = sbuf("aim_scaled", [P, I_TILES, G], F32)
        nc.vector.tensor_scalar(aim_scaled[:], aim_sb[:], -SLOPE, None, ALU.mult)

        i_tiles = [slice(h * P, (h + 1) * P) for h in range(I_TILES)]
        a_woven = sbuf("a_woven", [P, I, PACK], BF16)
        for cols in i_tiles:
            nc.vector.tensor_copy(a_woven[:, cols, :], a_picked[:, :, cols].rearrange("p t i -> p i t"))
        a_codes = sbuf("a_codes", [P, I], U32)
        a_scales = sbuf("a_scales", [P, I], U8)
        nc.vector.quantize_mx(out=a_codes[:].bitcast(FP8X4), scales=a_scales[:], in_=a_woven[:].rearrange("p i t -> p (i t)"))

        scores = [bank(number, "scores%d" % u, [P, 2, I]) for u, number in enumerate(SCORE_BANKS)]
        for t in range(PACK):
            nc.tensor.matmul_mx(
                out=scores[t // 2][:, t % 2, :],
                lhsT=dealt_words[:, t, :].bitcast(U8).bitcast(FP4X4),
                lhsT_scale=dealt_scales[:, t, :],
                rhs=a_codes[:].bitcast(FP8X4),
                rhs_scale=a_scales[:],
                start=True,
                stop=True,
            )

        squares = sbuf("squares", [P, PACK, I], F32)
        for u in range(len(scores)):
            nc.scalar.activation(squares[:, 2 * u : 2 * u + 2, :], scores[u][:], ACT.Square)
        square_sums = [bank(SUM_BANKS[h], "square_sums%d" % h, [P, P]) for h in range(I_TILES)]
        for t in range(PACK):
            for h in range(I_TILES):
                nc.tensor.matmul(
                    square_sums[h][:], squares[:, t, i_tiles[h]], identity[:], start=(t == 0), stop=(t == last), is_transpose=True
                )
        sums = sbuf("sums", [P, I_TILES, G], F32)
        for h in range(I_TILES):
            nc.vector.tensor_reduce(sums[:, h, :], square_sums[h][:].rearrange("p (g r) -> p g r", g=G), AXIS.X, ALU.add)
        scaled = sbuf("scaled", [P, PACK, I], F32)
        for t in range(PACK):
            nc.scalar.activation(scaled[:, t, :], scores[t // 2][:, t % 2, :], ACT.Copy, scale=js_cols[:, t : t + 1])
        inv_spread = sbuf("inv_spread", [P, I_TILES, G], F32)
        nc.scalar.activation(inv_spread[:], sums[:], ACT.Abs_reciprocal_sqrt, bias=EPSILON, scale=1.0 / GROUP)
        ratio_shape = [P, I_TILES * G, GROUP_ROWS]
        ratio = sbuf("ratio", ratio_shape, F32)
        nc.vector.tensor_tensor(
            ratio[:],
            inv_spread[:].rearrange("p h g -> p (h g)").unsqueeze(2).to_broadcast(ratio_shape),
            aim_scaled[:].rearrange("p h g -> p (h g)").unsqueeze(2).to_broadcast(ratio_shape),
            ALU.mult,
        )
        ratio_turned = bank(RATIO_BANK, "ratio_turned", [P, I])
        ratio_flat = ratio[:].rearrange("p c r -> p (c r)")
        for cols in i_tiles:
            nc.tensor.transpose(ratio_turned[:, cols], ratio_flat[:, cols], identity[:])

        g_woven = sbuf("g_woven", [P, I, PACK], BF16)
        for cols in i_tiles:
            nc.vector.scalar_tensor_tensor(
                g_woven[:, cols, :],
                ratio_turned[:, cols].unsqueeze(2).to_broadcast([P, P, PACK]),
                SLOPE,
                scaled[:, :, cols].rearrange("p t i -> p i t"),
                ALU.add,
                ALU.mult,
            )
        g_codes = sbuf("g_codes", [P, I], U32)
        g_scales = sbuf("g_scales", [P, I], U8)
        for cols in i_tiles:
            nc.vector.quantize_mx(
                out=g_codes[:, cols].bitcast(FP8X4), scales=g_scales[:, cols], in_=g_woven[:, cols, :].rearrange("p i t -> p (i t)")
            )

        bt_woven = [sbuf("bt_woven%d" % pair, [P, 2, P, 2], F32) for pair in range(D_TILES // 2)]
        bt_codes = sbuf("bt_codes", [P, D], U32, buffer_of="scaled")
        bt_scales = sbuf("bt_scales", [P, D], U8)
        for first, count, buffer_of, number in ((0, 2, None, 4), (2, 1, "sums", 5), (3, 1, "bt_woven0", 4)):
            picked = sbuf("b_picked%d" % first, [P, count, J], BF16, buffer_of=buffer_of)
            turned = bank(number, "b_turned%d" % first, [P, count, 2, P])
            for e in range(count):
                m = first + e
                if m % 2 == 1:
                    nc.vector.tensor_copy(picked[:, e, :], b_rows[m][:].indirect(idx2[:]))
                else:
                    nc.scalar.activation(picked[:, e, :], b_rows[m][:].indirect(idx2[:]), ACT.Copy)
            for e in range(count):
                words = picked[:, e, :].bitcast(F32)
                for u in range(2):
                    nc.tensor.transpose(turned[:, e, u, :], words[:, u : J // 2 : 2], identity[:])
            pair = first // 2
            nc.scalar.copy(bt_woven[pair][:, first % 2 : first % 2 + count], turned[:].rearrange("p e u d -> p e d u"))
            if (first + count) % 2 == 0:
                rows = slice(2 * pair * P, 2 * (pair + 1) * P)
                nc.vector.quantize_mx(
                    out=bt_codes[:, rows].bitcast(FP8X4),
                    scales=bt_scales[:, rows],
                    in_=bt_woven[pair][:].rearrange("p e d u -> p (e d u)").bitcast(BF16),
                )

        for m in range(D_TILES):
            grad = bank(GRAD_BANKS[m], "grad%d" % m, [P, I])
            rows = slice(m * P, (m + 1) * P)
            nc.tensor.matmul_mx(
                out=grad[:],
                lhsT=bt_codes[:, rows].bitcast(FP8X4),
                lhsT_scale=bt_scales[:, rows],
                rhs=g_codes[:].bitcast(FP8X4),
                rhs_scale=g_scales[:],
                start=True,
                stop=True,
            )
            grad_sb = sbuf("grad_sb%d" % m, [P, I], F32)
            nc.scalar.copy(grad_sb[:], grad[:])
            nc.scalar.activation(placed[m][:].indirect(idx[:]), grad_sb[:], ACT.Copy)

        faded = [sbuf("faded%d" % m, [P, T], F32) for m in range(D_TILES)]
        for m in range(D_TILES):
            for h in range(T_HALVES):
                cols = slice(h * BANK, (h + 1) * BANK)
                nc.vector.tensor_tensor(
                    faded[m][:, cols].rearrange("p (n c) -> p n c", c=PACK),
                    fade_rows[h][:].rearrange("p c n -> p n c"),
                    old_rows[m][:, cols].rearrange("p (n c) -> p n c", c=PACK),
                    ALU.mult,
                )
        for m in range(D_TILES):
            pieces = 2 if m == D_TILES - 1 else 1
            width = T // pieces
            for piece in range(pieces):
                cols = slice(piece * width, (piece + 1) * width)
                result = sbuf("result%d_%d" % (m, piece), [P, width], F32)
                nc.vector.tensor_tensor(result[:], faded[m][:, cols], placed[m][:, cols], ALU.add)
                nc.sync.dma_start(out[m * P : (m + 1) * P, cols], result[:])
